import numpy as np
import ml_dtypes


def mxq(x, axis, fmt="e4m3"):
    dtype, down = {"e4m3": (ml_dtypes.float8_e4m3fn, 7), "e5m2": (ml_dtypes.float8_e5m2, 14)}[fmt]
    v = np.moveaxis(np.asarray(x, np.float32).astype(ml_dtypes.bfloat16).astype(np.float64), axis, -1)
    blocks = v.reshape(v.shape[:-1] + (-1, 32))
    amax = np.abs(blocks).max(-1, keepdims=True)
    byte = np.maximum(np.where(amax > 0, np.frexp(amax)[1] - 1 + 127, 0) - down, 1)
    scale = np.exp2(byte - 127.0)
    codes = (blocks / scale).astype(np.float32).astype(dtype).astype(np.float64)
    return np.moveaxis((codes * scale).reshape(v.shape), -1, axis)


WIDE = False


def mx_kscale(k):
    if not WIDE:
        return np.ones(k)
    levels = np.array([30, -30])
    if k % 512:
        return np.exp2(np.random.permutation(np.resize(levels, k // 32))).repeat(32)
    a = np.empty((k // 512, 16))
    for p in range(k // 512):
        a[p, :8] = np.random.permutation(np.resize(levels, 8))
        for g in range(8):
            far = levels[np.abs(levels - a[p, g]) >= 10]
            a[p, g + 8] = far[np.random.randint(len(far))]
    return np.exp2(a.ravel()).repeat(32)


def f64(x):
    return np.asarray(x).astype(np.float64)


def striped(idx):
    return np.tile(np.asarray(idx).reshape(-1, 16).T, (8, 1)).astype(np.uint16)


def unstriped(offs):
    return offs[:16].T.reshape(-1).astype(np.int64)


E2M1 = np.array([0.0, 0.5, 1.0, 1.5, 2.0, 3.0, 4.0, 6.0, -0.0, -0.5, -1.0, -1.5, -2.0, -3.0, -4.0, -6.0])


def pack_weight(w, fmt):
    k, n = w.shape
    w = f64(np.asarray(w, np.float32).astype(ml_dtypes.bfloat16)).reshape(k // 32, 32, n)
    amax = np.abs(w).max(1)
    if fmt in ("e4m3", "e5m2"):
        byte = np.frexp(amax)[1] - 1 + 127 - (7 if fmt == "e4m3" else 14)
    else:
        mant, ex = np.frexp(amax / 6.0)
        byte = np.where(mant > 0.5, ex, ex - 1) + 127
    byte = np.clip(np.where(amax > 0, byte, 1), 1, 254)
    scaled = (w * np.exp2(127.0 - byte)[:, None, :]).reshape(k, n).astype(np.float32)
    by_word = np.ascontiguousarray(scaled.reshape(k // 512, 128, 4, n).transpose(0, 1, 3, 2))
    if fmt in ("e4m3", "e5m2"):
        words = by_word.astype(ml_dtypes.float8_e4m3fn if fmt == "e4m3" else ml_dtypes.float8_e5m2).view(np.uint8)
    else:
        c = by_word.astype(ml_dtypes.float4_e2m1fn).view(np.uint8) & 0xF
        words = (c[..., 0::2] | (c[..., 1::2] << 4)).reshape(k // 512, 128, 2 * n)
    return np.ascontiguousarray(words), np.ascontiguousarray(byte.astype(np.uint8).reshape(k // 512, 16, n))


def unpack_weight(words, scales, fmt):
    g, _, n = scales.shape
    words = np.ascontiguousarray(words).reshape(g, 128, n, -1)
    if fmt in ("e4m3", "e5m2"):
        vals = words.view(ml_dtypes.float8_e4m3fn if fmt == "e4m3" else ml_dtypes.float8_e5m2).astype(np.float64)
    else:
        nib = np.empty((g, 128, n, 4), np.uint8)
        nib[..., 0::2] = words & 0xF
        nib[..., 1::2] = words >> 4
        vals = E2M1[nib]
    vals = vals * np.repeat(np.exp2(scales.astype(np.float64) - 127.0), 8, axis=1)[..., None]
    return vals.transpose(0, 1, 3, 2).reshape(g * 512, n)


def e4m3fn_bytes(y):
    return np.clip(np.asarray(y, np.float64), -448.0, 448.0).astype(np.float32).astype(ml_dtypes.float8_e4m3fn).view(np.uint8)


def e4m3fn_values(b):
    return np.asarray(b, np.uint8).view(ml_dtypes.float8_e4m3fn).astype(np.float64)


def sgn(shape):
    return np.random.uniform(0.5, 2.0, shape) * np.where(np.random.standard_normal(shape) < 0, -1.0, 1.0)


K, T, J, R, F, Z, V, O, N = 512, 1024, 256, 512, 512, 1024, 512, 128, 256


def setup_inputs():
    n = np.random.standard_normal
    idx = np.random.permutation(T)[:J]
    idx2 = np.random.permutation(Z)[:J]
    idx3 = np.random.permutation(J)[:O]
    idx4 = np.random.permutation(V)[:O]
    idx5 = np.random.permutation(J)[:O]
    fk = mx_kscale(K)
    ff = mx_kscale(F)
    fr = mx_kscale(R)
    xtp = pack_weight(n((K, T)) / fk[:, None], "e2m1")
    xop = pack_weight(n((F, Z)) / ff[:, None], "e5m2")
    wp = pack_weight(n((K, R)) * 1 / np.sqrt(K) * fk[:, None] * fr, "e5m2")
    w2p = pack_weight(n((K, R)) * 1 / np.sqrt(K) * fk[:, None] * fr, "e4m3")
    w0p = pack_weight(n((F, R)) * 1 / np.sqrt(F) * ff[:, None] * fr, "e4m3")
    wbp = pack_weight(n((R, N)) * 1 / np.sqrt(R) / fr[:, None], "e4m3")
    return {
        "xt_words": xtp[0],
        "xt_scales": xtp[1],
        "xo_words": xop[0],
        "xo_scales": xop[1],
        "w_words": wp[0],
        "w_scales": wp[1],
        "w2_words": w2p[0],
        "w2_scales": w2p[1],
        "w0_words": w0p[0],
        "w0_scales": w0p[1],
        "ca": e4m3fn_bytes(60.0 * n((R, V))),
        "st": (np.random.uniform(0.008, 0.024, (R, 1)) * fr[:, None]).astype(np.float32),
        "sa": (sgn((R, 1))).astype(np.float32),
        "wb_words": wbp[0],
        "wb_scales": wbp[1],
        "offs": striped(idx),
        "offs2": striped(idx2),
        "offs3": striped(idx3),
        "offs4": striped(idx4),
        "offs5": striped(idx5),
    }


def reference(xt_words, xt_scales, xo_words, xo_scales, w_words, w_scales, w2_words, w2_scales, w0_words, w0_scales, ca, st, sa, wb_words, wb_scales, offs, offs2, offs3, offs4, offs5):
    idx = unstriped(offs)
    idx2 = unstriped(offs2)
    idx3 = unstriped(offs3)
    idx4 = unstriped(offs4)
    idx5 = unstriped(offs5)
    xtu = unpack_weight(xt_words, xt_scales, "e2m1")
    xou = unpack_weight(xo_words, xo_scales, "e5m2")
    wu = unpack_weight(w_words, w_scales, "e5m2")
    w2u = unpack_weight(w2_words, w2_scales, "e4m3")
    w0u = unpack_weight(w0_words, w0_scales, "e4m3")
    wbu = unpack_weight(wb_words, wb_scales, "e4m3")
    xtidxg = xtu[:, idx]
    a = wu.T @ xtidxg
    xoidx2g = xou[:, idx2]
    b = w2u.T @ xtidxg + w0u.T @ xoidx2g
    g1 = e4m3fn_values(ca)[:, idx4] * f64(st)
    hid = np.maximum(np.abs(a[:, idx3] * f64(sa) - g1), b[:, idx5])
    hidq = mxq(hid, 0, "e4m3")
    p = wbu.T @ hidq
    return p

@@ -1,0 +1,191 @@
+from contextlib import ExitStack
+
+import concourse.mybir as mybir
+
+F32 = mybir.dt.float32
+BF16 = mybir.dt.bfloat16
+I32 = mybir.dt.int32
+U32 = mybir.dt.uint32
+U16 = mybir.dt.uint16
+U8 = mybir.dt.uint8
+FP8 = mybir.dt.float8_e4m3fn
+E4M3 = mybir.dt.float8_e4m3fn_x4
+E5M2 = mybir.dt.float8_e5m2_x4
+E2M1 = mybir.dt.float4_e2m1fn_x4
+ALU = mybir.AluOpType
+ACT = mybir.ActivationFunctionType
+
+K, T, J, R, F, Z, V, O, N = 512, 1024, 256, 512, 512, 1024, 512, 128, 256
+P = 128
+PACK = 4
+FLOPS = 2 * (K * R * J * 2 + F * R * J + R * N * O)
+
+
+def tile_list_awayfrom_kernel(tc, xt_words, xt_scales, xo_words, xo_scales, w_words, w_scales, w2_words, w2_scales,
+                                    w0_words, w0_scales, ca, st, sa, wb_words, wb_scales, offs, offs2, offs3, offs4, offs5, out):
+    nc = tc.nc
+    with ExitStack() as ctx:
+        sb = ctx.enter_context(tc.tile_pool(name="sb", bufs=1))
+        ps = ctx.enter_context(tc.psum_pool(name="ps", bufs=1))
+
+        def tile(name, shape, dtype):
+            return sb.tile(shape, dtype, name=name, align_bytes=64)
+
+        def load_list(name, src):
+            t = tile(name, list(src.shape), U16)
+            nc.sync.dma_start(t[:], src)
+            return t
+
+        def zero_plane(name, width):
+            t = tile(name, [P, width], U8)
+            nc.vector.memset(t[:].bitcast(I32), 0)
+            return t
+
+        def load_plane(queue, plane, src):
+            for q in range(4):
+                queue.dma_start(plane[32 * q : 32 * q + 4, :].bitcast(I32), src[0, 4 * q : 4 * q + 4, :].bitcast(I32))
+
+        def load_words(name, src, width):
+            t = tile(name, [P, width], U32)
+            nc.sync.dma_start(t[:].bitcast(I32), src[0].rearrange("p n t -> p (n t)").bitcast(I32))
+            return t
+
+        def deal_words(name, raw, copy):
+            t = tile(name, [P, PACK, P], U32)
+            copy(t[:].rearrange("p t (c i) -> p c t i", i=4), raw[:].rearrange("p (c i t) -> p c t i", i=4, t=PACK))
+            return t
+
+        def deal_plane(name, raw):
+            t = tile(name, [P, PACK, P], U8)
+            nc.vector.tensor_copy(t[:], raw.rearrange("p (m t) -> p t m", t=PACK))
+            return t
+
+        def zero_stage(name, width, engine):
+            t = tile(name, [P, 2, width], U8)
+            engine.memset(t[:].bitcast(I32), 0)
+            return t
+
+        def load_stage(queue, stage, cols, src):
+            rows = src[0].rearrange("(h q r) n -> q r h n", h=2, q=2)
+            for q in range(2):
+                queue.dma_start(stage[32 * q : 32 * q + 4, :, cols].bitcast(I32), rows[q].bitcast(I32))
+
+        def spread(plane, stage):
+            for h in range(2):
+                nc.vector.tensor_copy(plane[64 * h : 64 * h + 64, :].bitcast(I32), stage[0:64, h, :].bitcast(I32))
+
+        def fold(stage):
+            nc.vector.tensor_copy(stage[64:128, 0, :].bitcast(I32), stage[0:64, 1, :].bitcast(I32))
+
+        xt_stage = zero_stage("xt_stage", T, nc.vector)
+        w_stage = zero_stage("w_stage", R, nc.gpsimd)
+        xo_stage = zero_stage("xo_stage", Z, nc.vector)
+        b_plane = zero_plane("b_plane", 2 * R)
+        b_rows = tile("b_rows", [4, 4, 2 * R], U8)
+        wb_plane = zero_plane("wb_plane", N)
+
+        sa_sb = tile("sa_sb", [P, PACK], F32)
+        st_sb = tile("st_sb", [P, PACK], F32)
+        nc.gpsimd.dma_start(sa_sb[:], sa.rearrange("(p t) o -> p (t o)", t=PACK))
+        nc.gpsimd.dma_start(st_sb[:], st.rearrange("(p t) o -> p (t o)", t=PACK))
+
+        idx = load_list("idx", offs)
+        xt_tab = tile("xt_tab", [P, T], U16)
+        nc.sync.dma_start(xt_tab[:].bitcast(I32), xt_words[0].bitcast(I32))
+        load_stage(nc.sync, xt_stage, slice(0, T), xt_scales)
+        w_raw = load_words("w_raw", w_words, R)
+        load_stage(nc.sync, w_stage, slice(0, R), w_scales)
+        w2_raw = load_words("w2_raw", w2_words, R)
+        xo_tab = load_words("xo_tab", xo_words, Z)
+        idx2 = load_list("idx2", offs2)
+        load_stage(nc.sync, xo_stage, slice(0, Z), xo_scales)
+        w0_raw = load_words("w0_raw", w0_words, R)
+        for cols, src in ((slice(0, R), w2_scales), (slice(R, 2 * R), w0_scales)):
+            nc.sync.dma_start(b_rows[:, :, cols].bitcast(I32), src[0].rearrange("(q r) n -> r q n", q=4).bitcast(I32))
+        idx4 = load_list("idx4", offs4)
+        idx3 = load_list("idx3", offs3)
+        ca_rows = ca.rearrange("(p t) v -> t p v", t=PACK)
+        ca_tab = [tile("ca_tab%d" % t, [P, V], U8) for t in range(PACK)]
+        for t in range(PACK):
+            nc.sync.dma_start(ca_tab[t][:], ca_rows[t])
+        idx5 = load_list("idx5", offs5)
+        wb_tab = load_words("wb_tab", wb_words, N)
+        load_plane(nc.sync, wb_plane, wb_scales)
+
+        xt_g = tile("xt_g", [P, J], U16)
+        xt_gs = tile("xt_gs", [P, J], U8)
+        xt_plane = tile("xt_plane", [P, T], U8)
+        nc.vector.tensor_copy(xt_g[:], xt_tab[:].indirect(idx[:]))
+        spread(xt_plane, xt_stage)
+        fold(w_stage)
+        nc.vector.tensor_copy(xt_gs[:], xt_plane[:].indirect(idx[:]))
+        w_d = deal_words("w_d", w_raw, nc.scalar.copy)
+        w_ds = deal_plane("w_ds", w_stage[:, 0, :])
+
+        a_ps = [ps.tile([P, J], F32, name="bank%d" % t) for t in range(PACK)]
+        a_sb = [tile("a_sb%d" % t, [P, J], F32) for t in range(PACK)]
+        a_g = tile("a_g", [P, PACK, O], F32)
+        for t in range(PACK):
+            nc.tensor.matmul_mx(a_ps[t][:], lhsT=w_d[:, t, :].bitcast(E5M2), lhsT_scale=w_ds[:, t, :],
+                                rhs=xt_g[:].bitcast(E2M1), rhs_scale=xt_gs[:], start=True, stop=True)
+        for t in range(PACK):
+            nc.scalar.activation(a_sb[t][:], a_ps[t][:], ACT.Copy)
+
+        xo_g = tile("xo_g", [P, J], U32)
+        xo_gs = tile("xo_gs", [P, J], U8)
+        xo_plane = tile("xo_plane", [P, Z], U8)
+        spread(xo_plane, xo_stage)
+        nc.vector.tensor_copy(xo_gs[:], xo_plane[:].indirect(idx2[:]))
+        nc.vector.tensor_copy(xo_g[:], xo_tab[:].indirect(idx2[:]))
+        for q in range(4):
+            nc.vector.tensor_copy(b_plane[32 * q : 32 * q + 4, :].bitcast(I32), b_rows[:, q, :].bitcast(I32))
+        w2_ds = deal_plane("w2_ds", b_plane[:, 0:R])
+        w0_ds = deal_plane("w0_ds", b_plane[:, R : 2 * R])
+        w2_d = deal_words("w2_d", w2_raw, nc.scalar.copy)
+        w0_d = deal_words("w0_d", w0_raw, nc.scalar.copy)
+
+        b_ps = [ps.tile([P, J], F32, name="bank%d" % (PACK + t)) for t in range(PACK)]
+        for t in range(PACK):
+            nc.tensor.matmul_mx(b_ps[t][:], lhsT=w2_d[:, t, :].bitcast(E4M3), lhsT_scale=w2_ds[:, t, :],
+                                rhs=xt_g[:].bitcast(E2M1), rhs_scale=xt_gs[:], start=True, stop=False)
+        for t in range(PACK):
+            nc.tensor.matmul_mx(b_ps[t][:], lhsT=w0_d[:, t, :].bitcast(E4M3), lhsT_scale=w0_ds[:, t, :],
+                                rhs=xo_g[:].bitcast(E5M2), rhs_scale=xo_gs[:], start=False, stop=True)
+
+        for t in range(PACK):
+            nc.scalar.activation(a_g[:, t, :], a_sb[t][:].indirect(idx3[:]), ACT.Copy, scale=sa_sb[:, t : t + 1])
+
+        ca_g = tile("ca_g", [P, PACK, O], U8)
+        g1 = tile("g1", [P, PACK, O], F32)
+        for t in range(PACK):
+            nc.vector.tensor_copy(ca_g[:, t, :], ca_tab[t][:].indirect(idx4[:]))
+        for t in range(PACK):
+            nc.vector.tensor_scalar(g1[:, t, :], ca_g[:, t, :].bitcast(FP8), st_sb[:, t : t + 1], None, ALU.mult)
+
+        diff = tile("diff", [P, PACK * O], F32)
+        mag = tile("mag", [P, PACK, O], F32)
+        nc.vector.tensor_tensor(diff[:], a_g[:].rearrange("p t o -> p (t o)"), g1[:].rearrange("p t o -> p (t o)"), ALU.subtract)
+        nc.vector.scalar_tensor_tensor(mag[:].rearrange("p t o -> p (t o)"), diff[:], -1.0, diff[:], ALU.mult, ALU.max)
+
+        b_sb = [tile("b_sb%d" % t, [P, J], F32) for t in range(PACK)]
+        b_g = tile("b_g", [P, PACK, O], F32)
+        for t in range(PACK):
+            nc.scalar.copy(b_sb[t][:], b_ps[t][:])
+        for t in range(PACK):
+            nc.scalar.activation(b_g[:, t, :], b_sb[t][:].indirect(idx5[:]), ACT.Copy)
+
+        hid = tile("hid", [P, O, PACK], BF16)
+        nc.vector.tensor_tensor(hid[:].rearrange("p (c i) t -> p c t i", i=4), mag[:].rearrange("p t (c i) -> p c t i", i=4),
+                                b_g[:].rearrange("p t (c i) -> p c t i", i=4), ALU.max)
+        hid_q = tile("hid_q", [P, O], U32)
+        hid_s = tile("hid_s", [P, O], U8)
+        nc.vector.quantize_mx(hid_q[:].bitcast(E4M3), hid_s[:], hid[:].rearrange("p o t -> p (o t)"))
+
+        for h, (copy, queue) in enumerate(((nc.vector.tensor_copy, nc.sync), (nc.scalar.copy, nc.scalar))):
+            cols = slice(h * P, (h + 1) * P)
+            o_ps = ps.tile([P, O], F32, name="bank%d" % h)
+            nc.tensor.matmul_mx(o_ps[:], lhsT=wb_tab[:, cols].bitcast(E4M3), lhsT_scale=wb_plane[:, cols],
+                                rhs=hid_q[:].bitcast(E4M3), rhs_scale=hid_s[:], start=True, stop=True)
+            o_sb = tile("o_sb%d" % h, [P, O], F32)
+            copy(o_sb[:], o_ps[:])
+            queue.dma_start(out[cols, :], o_sb[:])

@@ -28,8 +28,8 @@ def tile_list_awayfrom_kernel(tc, xt_words, xt_scales, xo_words, xo_scales, w_wo
         sb = ctx.enter_context(tc.tile_pool(name="sb", bufs=1))
         ps = ctx.enter_context(tc.psum_pool(name="ps", bufs=1))
 
-        def tile(name, shape, dtype):
-            return sb.tile(shape, dtype, name=name, align_bytes=64)
+        def tile(name, shape, dtype, tag=None):
+            return sb.tile(shape, dtype, name=name, tag=tag or name, align_bytes=64)
 
         def load_list(name, src):
             t = tile(name, list(src.shape), U16)
@@ -50,8 +50,8 @@ def tile_list_awayfrom_kernel(tc, xt_words, xt_scales, xo_words, xo_scales, w_wo
             nc.sync.dma_start(t[:].bitcast(I32), src[0].rearrange("p n t -> p (n t)").bitcast(I32))
             return t
 
-        def deal_words(name, raw, copy):
-            t = tile(name, [P, PACK, P], U32)
+        def deal_words(name, raw, copy, tag=None):
+            t = tile(name, [P, PACK, P], U32, tag)
             copy(t[:].rearrange("p t (c i) -> p c t i", i=4), raw[:].rearrange("p (c i t) -> p c t i", i=4, t=PACK))
             return t
 
@@ -60,50 +60,31 @@ def tile_list_awayfrom_kernel(tc, xt_words, xt_scales, xo_words, xo_scales, w_wo
             nc.vector.tensor_copy(t[:], raw.rearrange("p (m t) -> p t m", t=PACK))
             return t
 
-        def zero_stage(name, width, engine):
-            t = tile(name, [P, 2, width], U8)
-            engine.memset(t[:].bitcast(I32), 0)
-            return t
-
-        def load_stage(queue, stage, cols, src):
+        xt_plane = zero_plane("xt_plane", T)
+        w_plane = zero_plane("w_plane", R)
+        xo_plane = zero_plane("xo_plane", Z)
+        wb_plane = zero_plane("wb_plane", N)
+        b_stage = tile("b_stage", [P, 2, 2 * R], U8)
+        nc.gpsimd.memset(b_stage[:].bitcast(I32), 0)
+        for cols, src in ((slice(0, R), w2_scales), (slice(R, 2 * R), w0_scales)):
             rows = src[0].rearrange("(h q r) n -> q r h n", h=2, q=2)
             for q in range(2):
-                queue.dma_start(stage[32 * q : 32 * q + 4, :, cols].bitcast(I32), rows[q].bitcast(I32))
+                nc.gpsimd.dma_start(b_stage[32 * q : 32 * q + 4, :, cols].bitcast(I32), rows[q].bitcast(I32))
 
-        def spread(plane, stage):
-            for h in range(2):
-                nc.vector.tensor_copy(plane[64 * h : 64 * h + 64, :].bitcast(I32), stage[0:64, h, :].bitcast(I32))
-
-        def fold(stage):
-            nc.vector.tensor_copy(stage[64:128, 0, :].bitcast(I32), stage[0:64, 1, :].bitcast(I32))
-
-        xt_stage = zero_stage("xt_stage", T, nc.vector)
-        w_stage = zero_stage("w_stage", R, nc.gpsimd)
-        xo_stage = zero_stage("xo_stage", Z, nc.vector)
-        b_plane = zero_plane("b_plane", 2 * R)
-        b_rows = tile("b_rows", [4, 4, 2 * R], U8)
-        wb_plane = zero_plane("wb_plane", N)
-
-        sa_sb = tile("sa_sb", [P, PACK], F32)
-        st_sb = tile("st_sb", [P, PACK], F32)
-        nc.gpsimd.dma_start(sa_sb[:], sa.rearrange("(p t) o -> p (t o)", t=PACK))
-        nc.gpsimd.dma_start(st_sb[:], st.rearrange("(p t) o -> p (t o)", t=PACK))
+        load_plane(nc.scalar, xt_plane, xt_scales)
+        load_plane(nc.scalar, w_plane, w_scales)
 
         idx = load_list("idx", offs)
         xt_tab = tile("xt_tab", [P, T], U16)
         nc.sync.dma_start(xt_tab[:].bitcast(I32), xt_words[0].bitcast(I32))
-        load_stage(nc.sync, xt_stage, slice(0, T), xt_scales)
         w_raw = load_words("w_raw", w_words, R)
-        load_stage(nc.sync, w_stage, slice(0, R), w_scales)
-        w2_raw = load_words("w2_raw", w2_words, R)
         xo_tab = load_words("xo_tab", xo_words, Z)
         idx2 = load_list("idx2", offs2)
-        load_stage(nc.sync, xo_stage, slice(0, Z), xo_scales)
+        w2_raw = load_words("w2_raw", w2_words, R)
         w0_raw = load_words("w0_raw", w0_words, R)
-        for cols, src in ((slice(0, R), w2_scales), (slice(R, 2 * R), w0_scales)):
-            nc.sync.dma_start(b_rows[:, :, cols].bitcast(I32), src[0].rearrange("(q r) n -> r q n", q=4).bitcast(I32))
-        idx4 = load_list("idx4", offs4)
         idx3 = load_list("idx3", offs3)
+        load_plane(nc.sync, xo_plane, xo_scales)
+        idx4 = load_list("idx4", offs4)
         ca_rows = ca.rearrange("(p t) v -> t p v", t=PACK)
         ca_tab = [tile("ca_tab%d" % t, [P, V], U8) for t in range(PACK)]
         for t in range(PACK):
@@ -114,13 +95,14 @@ def tile_list_awayfrom_kernel(tc, xt_words, xt_scales, xo_words, xo_scales, w_wo
 
         xt_g = tile("xt_g", [P, J], U16)
         xt_gs = tile("xt_gs", [P, J], U8)
-        xt_plane = tile("xt_plane", [P, T], U8)
         nc.vector.tensor_copy(xt_g[:], xt_tab[:].indirect(idx[:]))
-        spread(xt_plane, xt_stage)
-        fold(w_stage)
         nc.vector.tensor_copy(xt_gs[:], xt_plane[:].indirect(idx[:]))
-        w_d = deal_words("w_d", w_raw, nc.scalar.copy)
-        w_ds = deal_plane("w_ds", w_stage[:, 0, :])
+        sa_sb = tile("sa_sb", [P, PACK], F32, "xt_tab")
+        st_sb = tile("st_sb", [P, PACK], F32, "xt_plane")
+        nc.gpsimd.dma_start(sa_sb[:], sa.rearrange("(p t) o -> p (t o)", t=PACK))
+        nc.gpsimd.dma_start(st_sb[:], st.rearrange("(p t) o -> p (t o)", t=PACK))
+        w_d = deal_words("w_d", w_raw, nc.vector.tensor_copy)
+        w_ds = deal_plane("w_ds", w_plane[:])
 
         a_ps = [ps.tile([P, J], F32, name="bank%d" % t) for t in range(PACK)]
         a_sb = [tile("a_sb%d" % t, [P, J], F32) for t in range(PACK)]
@@ -131,16 +113,15 @@ def tile_list_awayfrom_kernel(tc, xt_words, xt_scales, xo_words, xo_scales, w_wo
         for t in range(PACK):
             nc.scalar.activation(a_sb[t][:], a_ps[t][:], ACT.Copy)
 
-        xo_g = tile("xo_g", [P, J], U32)
+        xo_g = tile("xo_g", [P, J], U32, "w_plane")
         xo_gs = tile("xo_gs", [P, J], U8)
-        xo_plane = tile("xo_plane", [P, Z], U8)
-        spread(xo_plane, xo_stage)
-        nc.vector.tensor_copy(xo_gs[:], xo_plane[:].indirect(idx2[:]))
         nc.vector.tensor_copy(xo_g[:], xo_tab[:].indirect(idx2[:]))
-        for q in range(4):
-            nc.vector.tensor_copy(b_plane[32 * q : 32 * q + 4, :].bitcast(I32), b_rows[:, q, :].bitcast(I32))
+        b_plane = tile("b_plane", [P, 2 * R], U8, "xo_tab")
+        for h in range(2):
+            nc.vector.tensor_copy(b_plane[64 * h : 64 * h + 64, :].bitcast(I32), b_stage[0:64, h, :].bitcast(I32))
         w2_ds = deal_plane("w2_ds", b_plane[:, 0:R])
         w0_ds = deal_plane("w0_ds", b_plane[:, R : 2 * R])
+        nc.vector.tensor_copy(xo_gs[:], xo_plane[:].indirect(idx2[:]))
         w2_d = deal_words("w2_d", w2_raw, nc.scalar.copy)
         w0_d = deal_words("w0_d", w0_raw, nc.scalar.copy)
 
@@ -162,24 +143,31 @@ def tile_list_awayfrom_kernel(tc, xt_words, xt_scales, xo_words, xo_scales, w_wo
         for t in range(PACK):
             nc.vector.tensor_scalar(g1[:, t, :], ca_g[:, t, :].bitcast(FP8), st_sb[:, t : t + 1], None, ALU.mult)
 
-        diff = tile("diff", [P, PACK * O], F32)
+        halves = (slice(0, O // 2), slice(O // 2, O))
+        diff = tile("diff", [P, PACK, O], F32)
         mag = tile("mag", [P, PACK, O], F32)
-        nc.vector.tensor_tensor(diff[:], a_g[:].rearrange("p t o -> p (t o)"), g1[:].rearrange("p t o -> p (t o)"), ALU.subtract)
-        nc.vector.scalar_tensor_tensor(mag[:].rearrange("p t o -> p (t o)"), diff[:], -1.0, diff[:], ALU.mult, ALU.max)
+        for oh in halves:
+            nc.vector.tensor_tensor(diff[:, :, oh], a_g[:, :, oh], g1[:, :, oh], ALU.subtract)
+        for oh in halves:
+            nc.vector.scalar_tensor_tensor(mag[:, :, oh], diff[:, :, oh], -1.0, diff[:, :, oh], ALU.mult, ALU.max)
 
         b_sb = [tile("b_sb%d" % t, [P, J], F32) for t in range(PACK)]
         b_g = tile("b_g", [P, PACK, O], F32)
         for t in range(PACK):
             nc.scalar.copy(b_sb[t][:], b_ps[t][:])
-        for t in range(PACK):
+        for t in range(2):
             nc.scalar.activation(b_g[:, t, :], b_sb[t][:].indirect(idx5[:]), ACT.Copy)
+        for t in range(2, PACK):
+            nc.vector.tensor_copy(b_g[:, t, :], b_sb[t][:].indirect(idx5[:]))
 
         hid = tile("hid", [P, O, PACK], BF16)
-        nc.vector.tensor_tensor(hid[:].rearrange("p (c i) t -> p c t i", i=4), mag[:].rearrange("p t (c i) -> p c t i", i=4),
-                                b_g[:].rearrange("p t (c i) -> p c t i", i=4), ALU.max)
         hid_q = tile("hid_q", [P, O], U32)
         hid_s = tile("hid_s", [P, O], U8)
-        nc.vector.quantize_mx(hid_q[:].bitcast(E4M3), hid_s[:], hid[:].rearrange("p o t -> p (o t)"))
+        for oh in halves:
+            nc.vector.tensor_tensor(hid[:, oh, :].rearrange("p (c i) t -> p c t i", i=4), mag[:, :, oh].rearrange("p t (c i) -> p c t i", i=4),
+                                    b_g[:, :, oh].rearrange("p t (c i) -> p c t i", i=4), ALU.max)
+        for oh in halves:
+            nc.vector.quantize_mx(hid_q[:, oh].bitcast(E4M3), hid_s[:, oh], hid[:, oh, :].rearrange("p o t -> p (o t)"))
 
         for h, (copy, queue) in enumerate(((nc.vector.tensor_copy, nc.sync), (nc.scalar.copy, nc.scalar))):
             cols = slice(h * P, (h + 1) * P)

from contextlib import ExitStack

import concourse.mybir as mybir

F32 = mybir.dt.float32
BF16 = mybir.dt.bfloat16
I32 = mybir.dt.int32
U32 = mybir.dt.uint32
U16 = mybir.dt.uint16
U8 = mybir.dt.uint8
FP8 = mybir.dt.float8_e4m3fn
E4M3 = mybir.dt.float8_e4m3fn_x4
E5M2 = mybir.dt.float8_e5m2_x4
E2M1 = mybir.dt.float4_e2m1fn_x4
ALU = mybir.AluOpType
ACT = mybir.ActivationFunctionType

K, T, J, R, F, Z, V, O, N = 512, 1024, 256, 512, 512, 1024, 512, 128, 256
P = 128
PACK = 4
FLOPS = 2 * (K * R * J * 2 + F * R * J + R * N * O)


def tile_list_awayfrom_kernel(tc, xt_words, xt_scales, xo_words, xo_scales, w_words, w_scales, w2_words, w2_scales,
                                    w0_words, w0_scales, ca, st, sa, wb_words, wb_scales, offs, offs2, offs3, offs4, offs5, out):
    nc = tc.nc
    with ExitStack() as ctx:
        sb = ctx.enter_context(tc.tile_pool(name="sb", bufs=1))
        ps = ctx.enter_context(tc.psum_pool(name="ps", bufs=1))

        def tile(name, shape, dtype, tag=None):
            return sb.tile(shape, dtype, name=name, tag=tag or name, align_bytes=64)

        def load_list(name, src):
            t = tile(name, list(src.shape), U16)
            nc.sync.dma_start(t[:], src)
            return t

        def zero_plane(name, width):
            t = tile(name, [P, width], U8)
            nc.vector.memset(t[:].bitcast(I32), 0)
            return t

        def load_plane(queue, plane, src):
            for q in range(4):
                queue.dma_start(plane[32 * q : 32 * q + 4, :].bitcast(I32), src[0, 4 * q : 4 * q + 4, :].bitcast(I32))

        def load_words(name, src, width):
            t = tile(name, [P, width], U32)
            nc.sync.dma_start(t[:].bitcast(I32), src[0].rearrange("p n t -> p (n t)").bitcast(I32))
            return t

        def deal_words(name, raw, copy, tag=None):
            t = tile(name, [P, PACK, P], U32, tag)
            copy(t[:].rearrange("p t (c i) -> p c t i", i=4), raw[:].rearrange("p (c i t) -> p c t i", i=4, t=PACK))
            return t

        def deal_plane(name, raw):
            t = tile(name, [P, PACK, P], U8)
            nc.vector.tensor_copy(t[:], raw.rearrange("p (m t) -> p t m", t=PACK))
            return t

        xt_plane = zero_plane("xt_plane", T)
        w_plane = zero_plane("w_plane", R)
        xo_plane = zero_plane("xo_plane", Z)
        wb_plane = zero_plane("wb_plane", N)
        b_stage = tile("b_stage", [P, 2, 2 * R], U8)
        nc.gpsimd.memset(b_stage[:].bitcast(I32), 0)
        for cols, src in ((slice(0, R), w2_scales), (slice(R, 2 * R), w0_scales)):
            rows = src[0].rearrange("(h q r) n -> q r h n", h=2, q=2)
            for q in range(2):
                nc.gpsimd.dma_start(b_stage[32 * q : 32 * q + 4, :, cols].bitcast(I32), rows[q].bitcast(I32))

        load_plane(nc.scalar, xt_plane, xt_scales)
        load_plane(nc.scalar, w_plane, w_scales)

        idx = load_list("idx", offs)
        xt_tab = tile("xt_tab", [P, T], U16)
        nc.sync.dma_start(xt_tab[:].bitcast(I32), xt_words[0].bitcast(I32))
        w_raw = load_words("w_raw", w_words, R)
        xo_tab = load_words("xo_tab", xo_words, Z)
        idx2 = load_list("idx2", offs2)
        w2_raw = load_words("w2_raw", w2_words, R)
        w0_raw = load_words("w0_raw", w0_words, R)
        idx3 = load_list("idx3", offs3)
        load_plane(nc.sync, xo_plane, xo_scales)
        idx4 = load_list("idx4", offs4)
        ca_rows = ca.rearrange("(p t) v -> t p v", t=PACK)
        ca_tab = [tile("ca_tab%d" % t, [P, V], U8) for t in range(PACK)]
        for t in range(PACK):
            nc.sync.dma_start(ca_tab[t][:], ca_rows[t])
        idx5 = load_list("idx5", offs5)
        wb_tab = load_words("wb_tab", wb_words, N)
        load_plane(nc.sync, wb_plane, wb_scales)

        xt_g = tile("xt_g", [P, J], U16)
        xt_gs = tile("xt_gs", [P, J], U8)
        nc.vector.tensor_copy(xt_g[:], xt_tab[:].indirect(idx[:]))
        nc.vector.tensor_copy(xt_gs[:], xt_plane[:].indirect(idx[:]))
        sa_sb = tile("sa_sb", [P, PACK], F32, "xt_tab")
        st_sb = tile("st_sb", [P, PACK], F32, "xt_plane")
        nc.gpsimd.dma_start(sa_sb[:], sa.rearrange("(p t) o -> p (t o)", t=PACK))
        nc.gpsimd.dma_start(st_sb[:], st.rearrange("(p t) o -> p (t o)", t=PACK))
        w_d = deal_words("w_d", w_raw, nc.vector.tensor_copy)
        w_ds = deal_plane("w_ds", w_plane[:])

        a_ps = [ps.tile([P, J], F32, name="bank%d" % t) for t in range(PACK)]
        a_sb = [tile("a_sb%d" % t, [P, J], F32) for t in range(PACK)]
        a_g = tile("a_g", [P, PACK, O], F32)
        for t in range(PACK):
            nc.tensor.matmul_mx(a_ps[t][:], lhsT=w_d[:, t, :].bitcast(E5M2), lhsT_scale=w_ds[:, t, :],
                                rhs=xt_g[:].bitcast(E2M1), rhs_scale=xt_gs[:], start=True, stop=True)
        for t in range(PACK):
            nc.scalar.activation(a_sb[t][:], a_ps[t][:], ACT.Copy)

        xo_g = tile("xo_g", [P, J], U32, "w_plane")
        xo_gs = tile("xo_gs", [P, J], U8)
        nc.vector.tensor_copy(xo_g[:], xo_tab[:].indirect(idx2[:]))
        b_plane = tile("b_plane", [P, 2 * R], U8, "xo_tab")
        for h in range(2):
            nc.vector.tensor_copy(b_plane[64 * h : 64 * h + 64, :].bitcast(I32), b_stage[0:64, h, :].bitcast(I32))
        w2_ds = deal_plane("w2_ds", b_plane[:, 0:R])
        w0_ds = deal_plane("w0_ds", b_plane[:, R : 2 * R])
        nc.vector.tensor_copy(xo_gs[:], xo_plane[:].indirect(idx2[:]))
        w2_d = deal_words("w2_d", w2_raw, nc.scalar.copy)
        w0_d = deal_words("w0_d", w0_raw, nc.scalar.copy)

        b_ps = [ps.tile([P, J], F32, name="bank%d" % (PACK + t)) for t in range(PACK)]
        for t in range(PACK):
            nc.tensor.matmul_mx(b_ps[t][:], lhsT=w2_d[:, t, :].bitcast(E4M3), lhsT_scale=w2_ds[:, t, :],
                                rhs=xt_g[:].bitcast(E2M1), rhs_scale=xt_gs[:], start=True, stop=False)
        for t in range(PACK):
            nc.tensor.matmul_mx(b_ps[t][:], lhsT=w0_d[:, t, :].bitcast(E4M3), lhsT_scale=w0_ds[:, t, :],
                                rhs=xo_g[:].bitcast(E5M2), rhs_scale=xo_gs[:], start=False, stop=True)

        for t in range(PACK):
            nc.scalar.activation(a_g[:, t, :], a_sb[t][:].indirect(idx3[:]), ACT.Copy, scale=sa_sb[:, t : t + 1])

        ca_g = tile("ca_g", [P, PACK, O], U8)
        g1 = tile("g1", [P, PACK, O], F32)
        for t in range(PACK):
            nc.vector.tensor_copy(ca_g[:, t, :], ca_tab[t][:].indirect(idx4[:]))
        for t in range(PACK):
            nc.vector.tensor_scalar(g1[:, t, :], ca_g[:, t, :].bitcast(FP8), st_sb[:, t : t + 1], None, ALU.mult)

        halves = (slice(0, O // 2), slice(O // 2, O))
        diff = tile("diff", [P, PACK, O], F32)
        mag = tile("mag", [P, PACK, O], F32)
        for oh in halves:
            nc.vector.tensor_tensor(diff[:, :, oh], a_g[:, :, oh], g1[:, :, oh], ALU.subtract)
        for oh in halves:
            nc.vector.scalar_tensor_tensor(mag[:, :, oh], diff[:, :, oh], -1.0, diff[:, :, oh], ALU.mult, ALU.max)

        b_sb = [tile("b_sb%d" % t, [P, J], F32) for t in range(PACK)]
        b_g = tile("b_g", [P, PACK, O], F32)
        for t in range(PACK):
            nc.scalar.copy(b_sb[t][:], b_ps[t][:])
        for t in range(2):
            nc.scalar.activation(b_g[:, t, :], b_sb[t][:].indirect(idx5[:]), ACT.Copy)
        for t in range(2, PACK):
            nc.vector.tensor_copy(b_g[:, t, :], b_sb[t][:].indirect(idx5[:]))

        hid = tile("hid", [P, O, PACK], BF16)
        hid_q = tile("hid_q", [P, O], U32)
        hid_s = tile("hid_s", [P, O], U8)
        for oh in halves:
            nc.vector.tensor_tensor(hid[:, oh, :].rearrange("p (c i) t -> p c t i", i=4), mag[:, :, oh].rearrange("p t (c i) -> p c t i", i=4),
                                    b_g[:, :, oh].rearrange("p t (c i) -> p c t i", i=4), ALU.max)
        for oh in halves:
            nc.vector.quantize_mx(hid_q[:, oh].bitcast(E4M3), hid_s[:, oh], hid[:, oh, :].rearrange("p o t -> p (o t)"))

        for h, (copy, queue) in enumerate(((nc.vector.tensor_copy, nc.sync), (nc.scalar.copy, nc.scalar))):
            cols = slice(h * P, (h + 1) * P)
            o_ps = ps.tile([P, O], F32, name="bank%d" % h)
            nc.tensor.matmul_mx(o_ps[:], lhsT=wb_tab[:, cols].bitcast(E4M3), lhsT_scale=wb_plane[:, cols],
                                rhs=hid_q[:].bitcast(E4M3), rhs_scale=hid_s[:], start=True, stop=True)
            o_sb = tile("o_sb%d" % h, [P, O], F32)
            copy(o_sb[:], o_ps[:])
            queue.dma_start(out[cols, :], o_sb[:])
